import numpy as np
import ml_dtypes


def mxq(x, axis, fmt="e4m3"):
    dtype, down = {"e4m3": (ml_dtypes.float8_e4m3fn, 7), "e5m2": (ml_dtypes.float8_e5m2, 14)}[fmt]
    v = np.moveaxis(np.asarray(x, np.float32).astype(ml_dtypes.bfloat16).astype(np.float64), axis, -1)
    blocks = v.reshape(v.shape[:-1] + (-1, 32))
    amax = np.abs(blocks).max(-1, keepdims=True)
    byte = np.maximum(np.where(amax > 0, np.frexp(amax)[1] - 1 + 127, 0) - down, 1)
    scale = np.exp2(byte - 127.0)
    codes = (blocks / scale).astype(np.float32).astype(dtype).astype(np.float64)
    return np.moveaxis((codes * scale).reshape(v.shape), -1, axis)


WIDE = False


def mx_kscale(k):
    if not WIDE:
        return np.ones(k)
    levels = np.array([10, -10, 5, -5, 0])
    if k % 512:
        return np.exp2(np.random.permutation(np.resize(levels, k // 32))).repeat(32)
    a = np.empty((k // 512, 16))
    for p in range(k // 512):
        a[p, :8] = np.random.permutation(np.resize(levels, 8))
        for g in range(8):
            far = levels[np.abs(levels - a[p, g]) >= 10]
            a[p, g + 8] = far[np.random.randint(len(far))]
    return np.exp2(a.ravel()).repeat(32)


def f64(x):
    return np.asarray(x).astype(np.float64)


def striped(idx):
    return np.tile(idx.reshape(-1, 16).T, (8, 1)).astype(np.uint16)


def unstriped(offs):
    return offs[:16].T.reshape(-1).astype(np.int64)


def silu(v):
    return v / (1.0 + np.exp(-np.maximum(v, -700.0)))


K, T, E, C, H, N = 512, 1280, 8, 128, 512, 256


def by_expert(wq, xq):
    return np.concatenate([wq[e].T @ xq[:, e * C:(e + 1) * C] for e in range(E)], axis=1)


def setup_inputs():
    n = np.random.standard_normal
    s = mx_kscale(K)[:, None]
    u = mx_kscale(H)
    return {
        "xT": (n((K, T)) * s).astype(np.float32),
        "w1": (n((E, K, H)) / np.sqrt(K) / s[None]).astype(np.float32),
        "w3": (n((E, K, H)) / np.sqrt(K) / s[None] * u[None, None, :]).astype(np.float32),
        "w2": (n((E, H, N)) / np.sqrt(H) / u[None, :, None]).astype(np.float32),
        "gate": np.tile(np.random.uniform(0.2, 1.0, E * C), (K, 1)).astype(np.float32),
        "offs": striped(np.random.permutation(T)[:E * C]),
    }


def reference(xT, w1, w3, w2, gate, offs):
    idx = unstriped(offs)
    xq = mxq(f64(gate) * f64(xT)[:, idx], 0, "e4m3")
    h = silu(by_expert(mxq(f64(w1), 1, "e4m3"), xq))
    h = h * by_expert(mxq(f64(w3), 1, "e4m3"), xq)
    y = by_expert(mxq(f64(w2), 1, "e4m3"), mxq(h, 0, "e4m3"))
    out = np.zeros((N, T))
    out[:, idx] = y
    return out

@@ -1,0 +1,236 @@
+from contextlib import ExitStack
+
+import concourse.mybir as mybir
+from concourse.masks import make_identity
+
+K, T, E, C, H, N = 512, 1280, 8, 128, 512, 256
+S = E * C
+P = 128
+PACK = 4
+LANES = 16
+FLOPS = 2 * S * (2 * K * H + H * N)
+BYTES = 4 * (K * T + E * (2 * K * H + H * N) + S + N * T) + 2 * S
+
+F32 = mybir.dt.float32
+BF16 = mybir.dt.bfloat16
+U32 = mybir.dt.uint32
+U16 = mybir.dt.uint16
+U8 = mybir.dt.uint8
+FP8X4 = mybir.dt.float8_e4m3fn_x4
+MULT = mybir.AluOpType.mult
+COPY = mybir.ActivationFunctionType.Copy
+SILU = mybir.ActivationFunctionType.Silu
+
+HALF = S // 2
+GROUP = 2 * C
+PIECES = {
+    1: ((0, 0, 256),),
+    2: ((1, 0, 384),),
+    3: ((0, 256, 512),),
+    4: ((1, 384, 640),),
+    5: ((0, 512, 704),),
+    6: ((0, 704, 864), (1, 640, 864)),
+    7: ((0, 864, 1024), (1, 864, 1024)),
+}
+SHARED_UNTIL = 4
+W = 2 * P * PACK
+
+
+def tile_moe_pre_glu_silu_kernel(tc, xT, w1, w3, w2, gate, offs, out):
+    nc = tc.nc
+    with ExitStack() as ctx:
+        keep = ctx.enter_context(tc.tile_pool(name="keep", bufs=1))
+        raw = ctx.enter_context(tc.tile_pool(name="raw", bufs=1))
+        ring = ctx.enter_context(tc.tile_pool(name="ring", bufs=3))
+        psum_gate = ctx.enter_context(tc.psum_pool(name="psum_gate", bufs=1))
+        psum = ctx.enter_context(tc.psum_pool(name="psum", bufs=2))
+
+        def quantize(values, width, name, pool):
+            codes = pool.tile([P, width], U32, name=name + "_codes", align_bytes=64)
+            scales = pool.tile([P, width], U8, name=name + "_scales", align_bytes=64)
+            nc.vector.quantize_mx(out=codes[:].bitcast(FP8X4), scales=scales[:], in_=values)
+            return codes, scales
+
+        def multiply(result, stationary, cols, moving, slots):
+            nc.tensor.matmul_mx(
+                out=result,
+                lhsT=stationary[0][:, cols].bitcast(FP8X4),
+                lhsT_scale=stationary[1][:, cols],
+                rhs=moving[0][:, slots].bitcast(FP8X4),
+                rhs_scale=moving[1][:, slots],
+                start=True,
+                stop=True,
+            )
+
+        gate_cols = keep.tile([P, 2, PACK], F32, name="gate_cols")
+        nc.sync.dma_start(out=gate_cols[:], in_=gate[0].rearrange("(h n m) -> n h m", h=2, m=PACK))
+        offsets = keep.tile([P, S // LANES], U16, name="offsets")
+        nc.sync.dma_start(offsets[:], offs)
+        x_rows = xT.rearrange("(p j) c -> p j c", j=PACK)
+        planes = []
+        for j in range(PACK):
+            plane = keep.tile([P, T], F32, name="x_plane%d" % j)
+            nc.sync.dma_start(out=plane[:], in_=x_rows[:, j, :])
+            planes.append(plane)
+
+        identity = keep.tile([P, P], F32, name="identity")
+        make_identity(nc, identity[:])
+        windows = []
+        for b in range(N // P):
+            window = keep.tile([P, T], F32, name="window%d" % b)
+            nc.vector.memset(window[:], 0.0)
+            windows.append(window)
+
+        gate_banks = []
+        for h in range(2):
+            bank = psum_gate.tile([P, PACK, P], F32, name="gate_bank%d" % h)
+            for m in range(PACK):
+                nc.tensor.transpose(bank[:, m, :], gate_cols[:, h, m : m + 1].to_broadcast([P, P]), identity[:])
+            gate_banks.append(bank)
+        gate_first = keep.tile([P, HALF], F32, name="gate_first")
+        nc.vector.tensor_copy(
+            out=gate_first[:].rearrange("p (n m) -> p n m", m=PACK),
+            in_=gate_banks[0][:].rearrange("p m n -> p n m"),
+        )
+
+        gated = keep.tile([P, PACK, HALF], F32, name="gated")
+        plain = keep.tile([P, PACK, HALF], F32, name="plain")
+        for j in range(PACK):
+            nc.vector.tensor_tensor(
+                gated[:, j, :], planes[j][:].indirect(offsets[:, 0 : HALF // LANES]), gate_first[:], MULT
+            )
+            nc.scalar.activation(plain[:, j, :], planes[j][:].indirect(offsets[:, HALF // LANES : S // LANES]), COPY)
+
+        def tokens(g):
+            values = keep.tile([P, GROUP * PACK], BF16, name="x_bf%d" % g, align_bytes=64)
+            dst = values[:].rearrange("p (c i j) -> p c j i", i=PACK, j=PACK)
+            first = g * GROUP % HALF
+            if g * GROUP < HALF:
+                src = gated[:, :, first : first + GROUP].rearrange("p j (c i) -> p c j i", i=PACK)
+                nc.scalar.copy(out=dst, in_=src)
+            else:
+                src = plain[:, :, first : first + GROUP].rearrange("p j (c i) -> p c j i", i=PACK)
+                quads = slice(first // PACK, (first + GROUP) // PACK)
+                weight = gate_banks[1][:, :, quads].rearrange("p i c -> p c i")
+                weight = weight.unsqueeze(2).to_broadcast([P, GROUP // PACK, PACK, PACK])
+                nc.vector.tensor_tensor(dst, src, weight, MULT)
+            return values
+
+        def load(w, e, name, bufs):
+            loaded = raw.tile([P, PACK, w.shape[2]], F32, name=name, bufs=bufs)
+            nc.sync.dma_start(out=loaded[:], in_=w[e].rearrange("(p j) c -> p j c", j=PACK))
+            return loaded
+
+        def cast(engine, dst, src):
+            if engine == "scalar":
+                nc.scalar.copy(out=dst, in_=src)
+            else:
+                nc.vector.tensor_copy(out=dst, in_=src)
+
+        def cast_half(engine, values, loaded, half):
+            src = loaded[:].rearrange("p j (m t) -> p m j t", t=PACK)[:, :, :, 2 * half : 2 * half + 2]
+            cast(engine, values.rearrange("p (t m j) -> p m j t", t=2, j=PACK), src)
+
+        def first_layer(bank, half, weights, e):
+            for t in range(2):
+                multiply(
+                    bank[:, 2 * half + t, :],
+                    weights,
+                    slice(t * P, (t + 1) * P),
+                    x_mx[e // 2],
+                    slice(e % 2 * C, (e % 2 + 1) * C),
+                )
+
+        x_bf = [tokens(g) for g in range(S // GROUP)]
+        x_mx = {}
+        staged = keep.tile([P, N // P, S], F32, name="staged")
+        act, lin, h_mx, w2_raw, w2_bf = {}, {}, {}, {}, {}
+
+        def w1_casts(e, upper):
+            loaded = load(w1, e, "w13_raw", 9)
+            if e % 2 == 0:
+                x_mx[e // 2] = quantize(x_bf[e // 2][:], GROUP, "x%d" % (e // 2), keep)
+            lower = ring.tile([P, W], BF16, name="w1_lower", align_bytes=64)
+            cast_half("scalar" if e < SHARED_UNTIL else "vector", lower[:], loaded, 0)
+            cast_half("vector", upper, loaded, 1)
+            return lower
+
+        def activation(e, lower, upper_mx, room):
+            lower_mx = quantize(lower[:], 2 * P, "w1_lower", ring)
+            a = psum.tile([P, PACK, C], F32, name="a")
+            first_layer(a, 1, upper_mx, e)
+            first_layer(a, 0, lower_mx, e)
+            act[e] = room.rearrange("p (n t) -> p n t", t=PACK)
+            nc.scalar.activation(act[e], a[:].rearrange("p t n -> p n t"), SILU)
+
+        def w3_product(e, shared):
+            loaded = load(w3, e, "w13_raw", 9)
+            upper = ring.tile([P, W], BF16, name="w3_upper", align_bytes=64)
+            cast_half("vector", shared[:, W : 2 * W], loaded, 0)
+            cast_half("vector", upper[:], loaded, 1)
+            lower_mx = quantize(shared[:, W : 2 * W], 2 * P, "w3_lower", ring)
+            upper_mx = quantize(upper[:], 2 * P, "w3_upper", ring)
+            lin[e] = psum.tile([P, PACK, C], F32, name="lin")
+            first_layer(lin[e], 0, lower_mx, e)
+            first_layer(lin[e], 1, upper_mx, e)
+
+        def hidden(e, room):
+            nc.vector.tensor_tensor(
+                room.rearrange("p (n t) -> p n t", t=PACK), lin[e][:].rearrange("p t n -> p n t"), act[e], MULT
+            )
+
+        def w2_cast(e):
+            w2_raw[e] = load(w2, e, "w2_raw", 6)
+            w2_bf[e] = ring.tile([P, N * PACK], BF16, name="w2_bf", align_bytes=64)
+            cast(
+                "vector" if e == E - 1 else "scalar",
+                w2_bf[e][:].rearrange("p (c i j) -> p c j i", i=PACK, j=PACK),
+                w2_raw[e][:].rearrange("p j (c i) -> p c j i", i=PACK),
+            )
+
+        def second_layer(e):
+            w2_mx = quantize(w2_bf[e][:], N, "w2", ring)
+            y = psum.tile([P, N // P, C], F32, name="y")
+            codes, slots = h_mx[e]
+            for b in range(N // P):
+                multiply(y[:, b, :], w2_mx, slice(b * P, (b + 1) * P), codes, slots)
+            nc.scalar.copy(out=staged[:, :, e * C : (e + 1) * C], in_=y[:])
+            for b, lo, hi in PIECES.get(e, ()):
+                target = windows[b][:].indirect(offsets[:, lo // LANES : hi // LANES])
+                if e >= E - 2 and b == 0:
+                    nc.vector.tensor_copy(target, staged[:, b, lo:hi])
+                else:
+                    nc.scalar.activation(target, staged[:, b, lo:hi], COPY)
+
+        early_act = [keep.tile([P, C * PACK], F32, name="act%d" % e) for e in range(2)]
+        first_upper = keep.tile([P, W], BF16, name="first_upper", align_bytes=64)
+        lower = w1_casts(0, first_upper[:])
+        activation(0, lower, quantize(first_upper[:], 2 * P, "w1_upper0", keep), early_act[0][:])
+        for e in range(E):
+            shared = ring.tile([P, 2 * W], BF16, name="shared", align_bytes=64)
+            w3_product(e, shared)
+            behind = W + C * PACK
+            if e >= 1:
+                hidden(e - 1, shared[:, W:behind])
+            if e == 0:
+                lower = w1_casts(1, shared[:, 0:W])
+                activation(1, lower, quantize(shared[:, 0:W], 2 * P, "w1_upper1", keep), early_act[1][:])
+            elif e < E - 1:
+                lower = w1_casts(e + 1, shared[:, 0:W])
+                both_mx = quantize(shared[:, 0:behind], 2 * P + C, "both", ring)
+                h_mx[e - 1] = (both_mx, slice(2 * P, 2 * P + C))
+                w2_cast(e - 1)
+                room = w2_raw[e - 1][:, 0:2, :].rearrange("p j n -> p (j n)")
+                activation(e + 1, lower, both_mx, room)
+                second_layer(e - 1)
+            else:
+                hidden(e, shared[:, 0 : C * PACK])
+                h_mx[e - 1] = (quantize(shared[:, W:behind], C, "h_before", keep), slice(0, C))
+                h_mx[e] = (quantize(shared[:, 0 : C * PACK], C, "h_last", keep), slice(0, C))
+                w2_cast(e - 1)
+                w2_cast(e)
+                second_layer(e - 1)
+                second_layer(e)
+
+        for b in range(N // P):
+            nc.sync.dma_start(out=out[b * P : (b + 1) * P, :], in_=windows[b][:])

@@ -28,9 +28,9 @@ PIECES = {
     2: ((1, 0, 384),),
     3: ((0, 256, 512),),
     4: ((1, 384, 640),),
-    5: ((0, 512, 704),),
-    6: ((0, 704, 864), (1, 640, 864)),
-    7: ((0, 864, 1024), (1, 864, 1024)),
+    5: ((0, 512, 768),),
+    6: ((1, 640, 864),),
+    7: ((0, 768, 1024), (1, 864, 1024)),
 }
 SHARED_UNTIL = 4
 W = 2 * P * PACK
@@ -101,23 +101,22 @@ def tile_moe_pre_glu_silu_kernel(tc, xT, w1, w3, w2, gate, offs, out):
             )
             nc.scalar.activation(plain[:, j, :], planes[j][:].indirect(offsets[:, HALF // LANES : S // LANES]), COPY)
 
-        def tokens(g):
-            values = keep.tile([P, GROUP * PACK], BF16, name="x_bf%d" % g, align_bytes=64)
-            dst = values[:].rearrange("p (c i j) -> p c j i", i=PACK, j=PACK)
+        def tokens(g, values):
+            dst = values.rearrange("p (c i j) -> p c j i", i=PACK, j=PACK)
             first = g * GROUP % HALF
             if g * GROUP < HALF:
                 src = gated[:, :, first : first + GROUP].rearrange("p j (c i) -> p c j i", i=PACK)
-                nc.scalar.copy(out=dst, in_=src)
+                cast("vector" if g == 0 else "scalar", dst, src)
             else:
                 src = plain[:, :, first : first + GROUP].rearrange("p j (c i) -> p c j i", i=PACK)
                 quads = slice(first // PACK, (first + GROUP) // PACK)
                 weight = gate_banks[1][:, :, quads].rearrange("p i c -> p c i")
                 weight = weight.unsqueeze(2).to_broadcast([P, GROUP // PACK, PACK, PACK])
                 nc.vector.tensor_tensor(dst, src, weight, MULT)
-            return values
+            x_mx[g] = quantize(values, GROUP, "x%d" % g, keep)
 
         def load(w, e, name, bufs):
-            loaded = raw.tile([P, PACK, w.shape[2]], F32, name=name, bufs=bufs)
+            loaded = raw.tile([P, PACK, w.shape[2]], F32, name="weights_raw", bufs=12)
             nc.sync.dma_start(out=loaded[:], in_=w[e].rearrange("(p j) c -> p j c", j=PACK))
             return loaded
 
@@ -141,15 +140,15 @@ def tile_moe_pre_glu_silu_kernel(tc, xT, w1, w3, w2, gate, offs, out):
                     slice(e % 2 * C, (e % 2 + 1) * C),
                 )
 
-        x_bf = [tokens(g) for g in range(S // GROUP)]
         x_mx = {}
+        for g in range(2):
+            x_bf = keep.tile([P, W], BF16, name="x_bf%d" % g, align_bytes=64)
+            tokens(g, x_bf[:])
         staged = keep.tile([P, N // P, S], F32, name="staged")
         act, lin, h_mx, w2_raw, w2_bf = {}, {}, {}, {}, {}
 
         def w1_casts(e, upper):
             loaded = load(w1, e, "w13_raw", 9)
-            if e % 2 == 0:
-                x_mx[e // 2] = quantize(x_bf[e // 2][:], GROUP, "x%d" % (e // 2), keep)
             lower = ring.tile([P, W], BF16, name="w1_lower", align_bytes=64)
             cast_half("scalar" if e < SHARED_UNTIL else "vector", lower[:], loaded, 0)
             cast_half("vector", upper, loaded, 1)
@@ -190,47 +189,61 @@ def tile_moe_pre_glu_silu_kernel(tc, xT, w1, w3, w2, gate, offs, out):
 
         def second_layer(e):
             w2_mx = quantize(w2_bf[e][:], N, "w2", ring)
-            y = psum.tile([P, N // P, C], F32, name="y")
             codes, slots = h_mx[e]
-            for b in range(N // P):
-                multiply(y[:, b, :], w2_mx, slice(b * P, (b + 1) * P), codes, slots)
-            nc.scalar.copy(out=staged[:, :, e * C : (e + 1) * C], in_=y[:])
+            if e < E - 1:
+                y = psum.tile([P, N // P, C], F32, name="y")
+                for b in range(N // P):
+                    multiply(y[:, b, :], w2_mx, slice(b * P, (b + 1) * P), codes, slots)
+                nc.scalar.copy(out=staged[:, :, e * C : (e + 1) * C], in_=y[:])
+            else:
+                for b in range(N // P):
+                    y = psum.tile([P, N // P, C], F32, name="y")
+                    multiply(y[:, 0, :], w2_mx, slice(b * P, (b + 1) * P), codes, slots)
+                    cast("vector" if b == 0 else "scalar", staged[:, b, e * C : (e + 1) * C], y[:, 0, :])
             for b, lo, hi in PIECES.get(e, ()):
                 target = windows[b][:].indirect(offsets[:, lo // LANES : hi // LANES])
-                if e >= E - 2 and b == 0:
+                if e == E - 1 and b == 0:
                     nc.vector.tensor_copy(target, staged[:, b, lo:hi])
                 else:
                     nc.scalar.activation(target, staged[:, b, lo:hi], COPY)
 
-        early_act = [keep.tile([P, C * PACK], F32, name="act%d" % e) for e in range(2)]
-        first_upper = keep.tile([P, W], BF16, name="first_upper", align_bytes=64)
-        lower = w1_casts(0, first_upper[:])
-        activation(0, lower, quantize(first_upper[:], 2 * P, "w1_upper0", keep), early_act[0][:])
+        def early_w1(e):
+            upper = keep.tile([P, W], BF16, name="early_upper%d" % e, align_bytes=64)
+            room = keep.tile([P, C * PACK], F32, name="early_act%d" % e)
+            lower = w1_casts(e, upper[:])
+            activation(e, lower, quantize(upper[:], 2 * P, "early_upper%d" % e, keep), room[:])
+            tokens(2 + e, upper[:])
+
+        def late_hidden(e):
+            room = keep.tile([P, C * PACK], BF16, name="late_h%d" % e, align_bytes=64)
+            hidden(e, room[:])
+            return room
+
+        behind = W + C * PACK
+        early_w1(0)
         for e in range(E):
             shared = ring.tile([P, 2 * W], BF16, name="shared", align_bytes=64)
             w3_product(e, shared)
-            behind = W + C * PACK
-            if e >= 1:
+            if 1 <= e < E - 1:
                 hidden(e - 1, shared[:, W:behind])
+            if e >= E - 2:
+                late = late_hidden(e)
             if e == 0:
-                lower = w1_casts(1, shared[:, 0:W])
-                activation(1, lower, quantize(shared[:, 0:W], 2 * P, "w1_upper1", keep), early_act[1][:])
+                early_w1(1)
             elif e < E - 1:
                 lower = w1_casts(e + 1, shared[:, 0:W])
                 both_mx = quantize(shared[:, 0:behind], 2 * P + C, "both", ring)
                 h_mx[e - 1] = (both_mx, slice(2 * P, 2 * P + C))
-                w2_cast(e - 1)
+            if e >= E - 2:
+                h_mx[e] = (quantize(late[:], C, "late_h%d" % e, keep), slice(0, C))
+            ready = [f for f in (e - 1, e) if f in h_mx and f not in w2_raw]
+            for f in ready:
+                w2_cast(f)
+            if 1 <= e < E - 1:
                 room = w2_raw[e - 1][:, 0:2, :].rearrange("p j n -> p (j n)")
                 activation(e + 1, lower, both_mx, room)
-                second_layer(e - 1)
-            else:
-                hidden(e, shared[:, 0 : C * PACK])
-                h_mx[e - 1] = (quantize(shared[:, W:behind], C, "h_before", keep), slice(0, C))
-                h_mx[e] = (quantize(shared[:, 0 : C * PACK], C, "h_last", keep), slice(0, C))
-                w2_cast(e - 1)
-                w2_cast(e)
-                second_layer(e - 1)
-                second_layer(e)
+            for f in ready:
+                second_layer(f)
 
-        for b in range(N // P):
-            nc.sync.dma_start(out=out[b * P : (b + 1) * P, :], in_=windows[b][:])
+        nc.scalar.dma_start(out=out[P : 2 * P, :], in_=windows[1][:])
+        nc.sync.dma_start(out=out[0:P, :], in_=windows[0][:])

@@ -63,15 +63,16 @@ def tile_moe_pre_glu_silu_kernel(tc, xT, w1, w3, w2, gate, offs, out):
             )
 
         gate_cols = keep.tile([P, 2, PACK], F32, name="gate_cols")
-        nc.sync.dma_start(out=gate_cols[:], in_=gate[0].rearrange("(h n m) -> n h m", h=2, m=PACK))
+        nc.scalar.dma_start(out=gate_cols[:], in_=gate[0].rearrange("(h n m) -> n h m", h=2, m=PACK))
         offsets = keep.tile([P, S // LANES], U16, name="offsets")
-        nc.sync.dma_start(offsets[:], offs)
         x_rows = xT.rearrange("(p j) c -> p j c", j=PACK)
         planes = []
         for j in range(PACK):
             plane = keep.tile([P, T], F32, name="x_plane%d" % j)
             nc.sync.dma_start(out=plane[:], in_=x_rows[:, j, :])
             planes.append(plane)
+            if j == 0:
+                nc.sync.dma_start(offsets[:], offs)
 
         identity = keep.tile([P, P], F32, name="identity")
         make_identity(nc, identity[:])
@@ -166,7 +167,7 @@ def tile_moe_pre_glu_silu_kernel(tc, xT, w1, w3, w2, gate, offs, out):
             loaded = load(w3, e, "w13_raw", 9)
             upper = ring.tile([P, W], BF16, name="w3_upper", align_bytes=64)
             cast_half("vector", shared[:, W : 2 * W], loaded, 0)
-            cast_half("vector", upper[:], loaded, 1)
+            cast_half("scalar" if e < 2 else "vector", upper[:], loaded, 1)
             lower_mx = quantize(shared[:, W : 2 * W], 2 * P, "w3_lower", ring)
             upper_mx = quantize(upper[:], 2 * P, "w3_upper", ring)
             lin[e] = psum.tile([P, PACK, C], F32, name="lin")
@@ -196,7 +197,7 @@ def tile_moe_pre_glu_silu_kernel(tc, xT, w1, w3, w2, gate, offs, out):
                     multiply(y[:, b, :], w2_mx, slice(b * P, (b + 1) * P), codes, slots)
                 nc.scalar.copy(out=staged[:, :, e * C : (e + 1) * C], in_=y[:])
             else:
-                for b in range(N // P):
+                for b in reversed(range(N // P)):
                     y = psum.tile([P, N // P, C], F32, name="y")
                     multiply(y[:, 0, :], w2_mx, slice(b * P, (b + 1) * P), codes, slots)
                     cast("vector" if b == 0 else "scalar", staged[:, b, e * C : (e + 1) * C], y[:, 0, :])

from contextlib import ExitStack

import concourse.mybir as mybir
from concourse.masks import make_identity

K, T, E, C, H, N = 512, 1280, 8, 128, 512, 256
S = E * C
P = 128
PACK = 4
LANES = 16
FLOPS = 2 * S * (2 * K * H + H * N)
BYTES = 4 * (K * T + E * (2 * K * H + H * N) + S + N * T) + 2 * S

F32 = mybir.dt.float32
BF16 = mybir.dt.bfloat16
U32 = mybir.dt.uint32
U16 = mybir.dt.uint16
U8 = mybir.dt.uint8
FP8X4 = mybir.dt.float8_e4m3fn_x4
MULT = mybir.AluOpType.mult
COPY = mybir.ActivationFunctionType.Copy
SILU = mybir.ActivationFunctionType.Silu

HALF = S // 2
GROUP = 2 * C
PIECES = {
    1: ((0, 0, 256),),
    2: ((1, 0, 384),),
    3: ((0, 256, 512),),
    4: ((1, 384, 640),),
    5: ((0, 512, 768),),
    6: ((1, 640, 864),),
    7: ((0, 768, 1024), (1, 864, 1024)),
}
SHARED_UNTIL = 4
W = 2 * P * PACK


def tile_moe_pre_glu_silu_kernel(tc, xT, w1, w3, w2, gate, offs, out):
    nc = tc.nc
    with ExitStack() as ctx:
        keep = ctx.enter_context(tc.tile_pool(name="keep", bufs=1))
        raw = ctx.enter_context(tc.tile_pool(name="raw", bufs=1))
        ring = ctx.enter_context(tc.tile_pool(name="ring", bufs=3))
        psum_gate = ctx.enter_context(tc.psum_pool(name="psum_gate", bufs=1))
        psum = ctx.enter_context(tc.psum_pool(name="psum", bufs=2))

        def quantize(values, width, name, pool):
            codes = pool.tile([P, width], U32, name=name + "_codes", align_bytes=64)
            scales = pool.tile([P, width], U8, name=name + "_scales", align_bytes=64)
            nc.vector.quantize_mx(out=codes[:].bitcast(FP8X4), scales=scales[:], in_=values)
            return codes, scales

        def multiply(result, stationary, cols, moving, slots):
            nc.tensor.matmul_mx(
                out=result,
                lhsT=stationary[0][:, cols].bitcast(FP8X4),
                lhsT_scale=stationary[1][:, cols],
                rhs=moving[0][:, slots].bitcast(FP8X4),
                rhs_scale=moving[1][:, slots],
                start=True,
                stop=True,
            )

        gate_cols = keep.tile([P, 2, PACK], F32, name="gate_cols")
        nc.scalar.dma_start(out=gate_cols[:], in_=gate[0].rearrange("(h n m) -> n h m", h=2, m=PACK))
        offsets = keep.tile([P, S // LANES], U16, name="offsets")
        x_rows = xT.rearrange("(p j) c -> p j c", j=PACK)
        planes = []
        for j in range(PACK):
            plane = keep.tile([P, T], F32, name="x_plane%d" % j)
            nc.sync.dma_start(out=plane[:], in_=x_rows[:, j, :])
            planes.append(plane)
            if j == 0:
                nc.sync.dma_start(offsets[:], offs)

        identity = keep.tile([P, P], F32, name="identity")
        make_identity(nc, identity[:])
        windows = []
        for b in range(N // P):
            window = keep.tile([P, T], F32, name="window%d" % b)
            nc.vector.memset(window[:], 0.0)
            windows.append(window)

        gate_banks = []
        for h in range(2):
            bank = psum_gate.tile([P, PACK, P], F32, name="gate_bank%d" % h)
            for m in range(PACK):
                nc.tensor.transpose(bank[:, m, :], gate_cols[:, h, m : m + 1].to_broadcast([P, P]), identity[:])
            gate_banks.append(bank)
        gate_first = keep.tile([P, HALF], F32, name="gate_first")
        nc.vector.tensor_copy(
            out=gate_first[:].rearrange("p (n m) -> p n m", m=PACK),
            in_=gate_banks[0][:].rearrange("p m n -> p n m"),
        )

        gated = keep.tile([P, PACK, HALF], F32, name="gated")
        plain = keep.tile([P, PACK, HALF], F32, name="plain")
        for j in range(PACK):
            nc.vector.tensor_tensor(
                gated[:, j, :], planes[j][:].indirect(offsets[:, 0 : HALF // LANES]), gate_first[:], MULT
            )
            nc.scalar.activation(plain[:, j, :], planes[j][:].indirect(offsets[:, HALF // LANES : S // LANES]), COPY)

        def tokens(g, values):
            dst = values.rearrange("p (c i j) -> p c j i", i=PACK, j=PACK)
            first = g * GROUP % HALF
            if g * GROUP < HALF:
                src = gated[:, :, first : first + GROUP].rearrange("p j (c i) -> p c j i", i=PACK)
                cast("vector" if g == 0 else "scalar", dst, src)
            else:
                src = plain[:, :, first : first + GROUP].rearrange("p j (c i) -> p c j i", i=PACK)
                quads = slice(first // PACK, (first + GROUP) // PACK)
                weight = gate_banks[1][:, :, quads].rearrange("p i c -> p c i")
                weight = weight.unsqueeze(2).to_broadcast([P, GROUP // PACK, PACK, PACK])
                nc.vector.tensor_tensor(dst, src, weight, MULT)
            x_mx[g] = quantize(values, GROUP, "x%d" % g, keep)

        def load(w, e, name, bufs):
            loaded = raw.tile([P, PACK, w.shape[2]], F32, name="weights_raw", bufs=12)
            nc.sync.dma_start(out=loaded[:], in_=w[e].rearrange("(p j) c -> p j c", j=PACK))
            return loaded

        def cast(engine, dst, src):
            if engine == "scalar":
                nc.scalar.copy(out=dst, in_=src)
            else:
                nc.vector.tensor_copy(out=dst, in_=src)

        def cast_half(engine, values, loaded, half):
            src = loaded[:].rearrange("p j (m t) -> p m j t", t=PACK)[:, :, :, 2 * half : 2 * half + 2]
            cast(engine, values.rearrange("p (t m j) -> p m j t", t=2, j=PACK), src)

        def first_layer(bank, half, weights, e):
            for t in range(2):
                multiply(
                    bank[:, 2 * half + t, :],
                    weights,
                    slice(t * P, (t + 1) * P),
                    x_mx[e // 2],
                    slice(e % 2 * C, (e % 2 + 1) * C),
                )

        x_mx = {}
        for g in range(2):
            x_bf = keep.tile([P, W], BF16, name="x_bf%d" % g, align_bytes=64)
            tokens(g, x_bf[:])
        staged = keep.tile([P, N // P, S], F32, name="staged")
        act, lin, h_mx, w2_raw, w2_bf = {}, {}, {}, {}, {}

        def w1_casts(e, upper):
            loaded = load(w1, e, "w13_raw", 9)
            lower = ring.tile([P, W], BF16, name="w1_lower", align_bytes=64)
            cast_half("scalar" if e < SHARED_UNTIL else "vector", lower[:], loaded, 0)
            cast_half("vector", upper, loaded, 1)
            return lower

        def activation(e, lower, upper_mx, room):
            lower_mx = quantize(lower[:], 2 * P, "w1_lower", ring)
            a = psum.tile([P, PACK, C], F32, name="a")
            first_layer(a, 1, upper_mx, e)
            first_layer(a, 0, lower_mx, e)
            act[e] = room.rearrange("p (n t) -> p n t", t=PACK)
            nc.scalar.activation(act[e], a[:].rearrange("p t n -> p n t"), SILU)

        def w3_product(e, shared):
            loaded = load(w3, e, "w13_raw", 9)
            upper = ring.tile([P, W], BF16, name="w3_upper", align_bytes=64)
            cast_half("vector", shared[:, W : 2 * W], loaded, 0)
            cast_half("scalar" if e < 2 else "vector", upper[:], loaded, 1)
            lower_mx = quantize(shared[:, W : 2 * W], 2 * P, "w3_lower", ring)
            upper_mx = quantize(upper[:], 2 * P, "w3_upper", ring)
            lin[e] = psum.tile([P, PACK, C], F32, name="lin")
            first_layer(lin[e], 0, lower_mx, e)
            first_layer(lin[e], 1, upper_mx, e)

        def hidden(e, room):
            nc.vector.tensor_tensor(
                room.rearrange("p (n t) -> p n t", t=PACK), lin[e][:].rearrange("p t n -> p n t"), act[e], MULT
            )

        def w2_cast(e):
            w2_raw[e] = load(w2, e, "w2_raw", 6)
            w2_bf[e] = ring.tile([P, N * PACK], BF16, name="w2_bf", align_bytes=64)
            cast(
                "vector" if e == E - 1 else "scalar",
                w2_bf[e][:].rearrange("p (c i j) -> p c j i", i=PACK, j=PACK),
                w2_raw[e][:].rearrange("p j (c i) -> p c j i", i=PACK),
            )

        def second_layer(e):
            w2_mx = quantize(w2_bf[e][:], N, "w2", ring)
            codes, slots = h_mx[e]
            if e < E - 1:
                y = psum.tile([P, N // P, C], F32, name="y")
                for b in range(N // P):
                    multiply(y[:, b, :], w2_mx, slice(b * P, (b + 1) * P), codes, slots)
                nc.scalar.copy(out=staged[:, :, e * C : (e + 1) * C], in_=y[:])
            else:
                for b in reversed(range(N // P)):
                    y = psum.tile([P, N // P, C], F32, name="y")
                    multiply(y[:, 0, :], w2_mx, slice(b * P, (b + 1) * P), codes, slots)
                    cast("vector" if b == 0 else "scalar", staged[:, b, e * C : (e + 1) * C], y[:, 0, :])
            for b, lo, hi in PIECES.get(e, ()):
                target = windows[b][:].indirect(offsets[:, lo // LANES : hi // LANES])
                if e == E - 1 and b == 0:
                    nc.vector.tensor_copy(target, staged[:, b, lo:hi])
                else:
                    nc.scalar.activation(target, staged[:, b, lo:hi], COPY)

        def early_w1(e):
            upper = keep.tile([P, W], BF16, name="early_upper%d" % e, align_bytes=64)
            room = keep.tile([P, C * PACK], F32, name="early_act%d" % e)
            lower = w1_casts(e, upper[:])
            activation(e, lower, quantize(upper[:], 2 * P, "early_upper%d" % e, keep), room[:])
            tokens(2 + e, upper[:])

        def late_hidden(e):
            room = keep.tile([P, C * PACK], BF16, name="late_h%d" % e, align_bytes=64)
            hidden(e, room[:])
            return room

        behind = W + C * PACK
        early_w1(0)
        for e in range(E):
            shared = ring.tile([P, 2 * W], BF16, name="shared", align_bytes=64)
            w3_product(e, shared)
            if 1 <= e < E - 1:
                hidden(e - 1, shared[:, W:behind])
            if e >= E - 2:
                late = late_hidden(e)
            if e == 0:
                early_w1(1)
            elif e < E - 1:
                lower = w1_casts(e + 1, shared[:, 0:W])
                both_mx = quantize(shared[:, 0:behind], 2 * P + C, "both", ring)
                h_mx[e - 1] = (both_mx, slice(2 * P, 2 * P + C))
            if e >= E - 2:
                h_mx[e] = (quantize(late[:], C, "late_h%d" % e, keep), slice(0, C))
            ready = [f for f in (e - 1, e) if f in h_mx and f not in w2_raw]
            for f in ready:
                w2_cast(f)
            if 1 <= e < E - 1:
                room = w2_raw[e - 1][:, 0:2, :].rearrange("p j n -> p (j n)")
                activation(e + 1, lower, both_mx, room)
            for f in ready:
                second_layer(f)

        nc.scalar.dma_start(out=out[P : 2 * P, :], in_=windows[1][:])
        nc.sync.dma_start(out=out[0:P, :], in_=windows[0][:])
